import numpy as np
import ml_dtypes

BF16 = ml_dtypes.bfloat16


def bf(x):
    return np.asarray(x, np.float32).astype(BF16)


def f32(x):
    return np.asarray(x, np.float32)


def f64(x):
    return np.asarray(x).astype(np.float64)


def striped(idx):
    return np.concatenate([l.reshape(-1, 16).T for l in idx])


def rows(idx, k):
    return np.tile(np.repeat(idx, 16, axis=0), (k // (16 * 8), 1))


def look(tab, idx):
    return np.take_along_axis(f64(tab), rows(idx, len(tab)), axis=1)


K, S, D, V, N, M = 256, 2048, 2, 512, 1024, 256


def setup_inputs():
    return {"tab": f32(np.random.standard_normal((K, S))), "x0": f32(np.random.standard_normal((K, V))), "w": bf(np.random.standard_normal((K, M)) / np.sqrt(K)), "b": f32(0.5 * np.random.standard_normal((M, 1))), "offs": striped(np.stack([np.random.permutation(S)[:N] for _ in range(8)]))}


def reference(tab, x0, w, b, offs):
    idx = np.stack([g.T.reshape(-1) for g in np.split(offs, 8)])
    x = f64(x0)
    for d in range(D):
        x = np.maximum(x, look(tab, idx[:, d * V:(d + 1) * V]))
    y = f64(w).T @ x
    return np.maximum(y + f64(b), 0.0)

@@ -1,0 +1,60 @@
+import concourse.mybir as mybir
+
+F32, BF16, U16 = mybir.dt.float32, mybir.dt.bfloat16, mybir.dt.uint16
+ALU = mybir.AluOpType
+ACT = mybir.ActivationFunctionType
+
+P = 128
+GROUP = 16
+FLOPS = 2 * 256 * 256 * 512
+
+
+def tile_lookup_pool_max_relu_kernel(tc, tab, x0, w, b, offs, out):
+    nc = tc.nc
+    rows, width = tab.shape
+    points = x0.shape[1]
+    features = w.shape[1]
+    row_blocks, feature_blocks = rows // P, features // P
+    piece_cols = points // GROUP
+    neighbours = offs.shape[1] // piece_cols
+
+    with (
+        tc.tile_pool(name="held", bufs=1) as held,
+        tc.psum_pool(name="psum", bufs=1) as psum,
+    ):
+        offsets = held.tile([P, offs.shape[1]], U16, name="offsets")
+        nc.sync.dma_start(offsets[:], offs)
+        windows, centres = [], []
+        for r in range(row_blocks):
+            window = held.tile([P, width], F32, name=f"window{r}")
+            centre = held.tile([P, points], F32, name=f"centre{r}")
+            nc.sync.dma_start(window[:], tab[r * P:(r + 1) * P, :])
+            nc.sync.dma_start(centre[:], x0[r * P:(r + 1) * P, :])
+            windows.append(window)
+            centres.append(centre)
+        weights = held.tile([P, row_blocks, features], BF16, name="weights")
+        nc.sync.dma_start(weights[:], w.rearrange("(r p) m -> p r m", p=P))
+        biases = []
+        for m in range(feature_blocks):
+            bias = held.tile([P, 1], F32, name=f"bias{m}")
+            nc.sync.dma_start(bias[:], b[m * P:(m + 1) * P, :])
+            biases.append(bias)
+
+        products = [psum.tile([P, points], F32, name=f"product{m}") for m in range(feature_blocks)]
+        for r in range(row_blocks):
+            running = centres[r]
+            for d in range(neighbours):
+                larger = held.tile([P, points], F32, name=f"larger{r}_{d}")
+                picked = windows[r][:].indirect(offsets[:, d * piece_cols:(d + 1) * piece_cols])
+                nc.vector.tensor_tensor(larger[:], picked, running[:], ALU.max)
+                running = larger
+            pooled = held.tile([P, points], BF16, name=f"pooled{r}")
+            nc.scalar.copy(pooled[:], running[:])
+            for m in range(feature_blocks):
+                nc.tensor.matmul(products[m][:], weights[:, r, m * P:(m + 1) * P], pooled[:],
+                                 start=(r == 0), stop=(r == row_blocks - 1))
+
+        for m in range(feature_blocks):
+            result = held.tile([P, points], F32, name=f"result{m}")
+            nc.scalar.activation(result[:], products[m][:], ACT.Relu, bias=biases[m][:])
+            nc.sync.dma_start(out[m * P:(m + 1) * P, :], result[:])

@@ -6,6 +6,7 @@ ACT = mybir.ActivationFunctionType
 
 P = 128
 GROUP = 16
+HALVES = 2
 FLOPS = 2 * 256 * 256 * 512
 
 
@@ -18,20 +19,22 @@ def tile_lookup_pool_max_relu_kernel(tc, tab, x0, w, b, offs, out):
     piece_cols = points // GROUP
     neighbours = offs.shape[1] // piece_cols
 
+    half = points // HALVES
+    last_block = row_blocks - 1
+
     with (
         tc.tile_pool(name="held", bufs=1) as held,
         tc.psum_pool(name="psum", bufs=1) as psum,
     ):
+        windows = [held.tile([P, width], F32, name=f"window{r}") for r in range(row_blocks)]
+        centres = [held.tile([P, points], F32, name=f"centre{r}") for r in range(row_blocks)]
         offsets = held.tile([P, offs.shape[1]], U16, name="offsets")
+        nc.sync.dma_start(windows[0][:], tab[0:P, :])
         nc.sync.dma_start(offsets[:], offs)
-        windows, centres = [], []
-        for r in range(row_blocks):
-            window = held.tile([P, width], F32, name=f"window{r}")
-            centre = held.tile([P, points], F32, name=f"centre{r}")
-            nc.sync.dma_start(window[:], tab[r * P:(r + 1) * P, :])
-            nc.sync.dma_start(centre[:], x0[r * P:(r + 1) * P, :])
-            windows.append(window)
-            centres.append(centre)
+        nc.sync.dma_start(centres[0][:], x0[0:P, :])
+        for r in range(1, row_blocks):
+            nc.sync.dma_start(windows[r][:], tab[r * P:(r + 1) * P, :])
+            nc.sync.dma_start(centres[r][:], x0[r * P:(r + 1) * P, :])
         weights = held.tile([P, row_blocks, features], BF16, name="weights")
         nc.sync.dma_start(weights[:], w.rearrange("(r p) m -> p r m", p=P))
         biases = []
@@ -40,7 +43,8 @@ def tile_lookup_pool_max_relu_kernel(tc, tab, x0, w, b, offs, out):
             nc.sync.dma_start(bias[:], b[m * P:(m + 1) * P, :])
             biases.append(bias)
 
-        products = [psum.tile([P, points], F32, name=f"product{m}") for m in range(feature_blocks)]
+        products = [[psum.tile([P, half], F32, name=f"product{h}_{m}") for m in range(feature_blocks)]
+                    for h in range(HALVES)]
         for r in range(row_blocks):
             running = centres[r]
             for d in range(neighbours):
@@ -48,13 +52,22 @@ def tile_lookup_pool_max_relu_kernel(tc, tab, x0, w, b, offs, out):
                 picked = windows[r][:].indirect(offsets[:, d * piece_cols:(d + 1) * piece_cols])
                 nc.vector.tensor_tensor(larger[:], picked, running[:], ALU.max)
                 running = larger
-            pooled = held.tile([P, points], BF16, name=f"pooled{r}")
-            nc.scalar.copy(pooled[:], running[:])
-            for m in range(feature_blocks):
-                nc.tensor.matmul(products[m][:], weights[:, r, m * P:(m + 1) * P], pooled[:],
-                                 start=(r == 0), stop=(r == row_blocks - 1))
+            for h in range(HALVES):
+                pooled = held.tile([P, half], BF16, name=f"pooled{r}_{h}")
+                source = running[:, h * half:(h + 1) * half]
+                if r == last_block:
+                    nc.vector.tensor_copy(pooled[:], source)
+                else:
+                    nc.scalar.copy(pooled[:], source)
+                for m in range(feature_blocks):
+                    nc.tensor.matmul(products[h][m][:], weights[:, r, m * P:(m + 1) * P], pooled[:],
+                                     start=(r == 0), stop=(r == last_block))
 
-        for m in range(feature_blocks):
-            result = held.tile([P, points], F32, name=f"result{m}")
-            nc.scalar.activation(result[:], products[m][:], ACT.Relu, bias=biases[m][:])
-            nc.sync.dma_start(out[m * P:(m + 1) * P, :], result[:])
+        for h in range(HALVES):
+            for m in range(feature_blocks):
+                result = held.tile([P, half], F32, name=f"result{h}_{m}")
+                if m % 2 == 0:
+                    nc.scalar.activation(result[:], products[h][m][:], ACT.Relu, bias=biases[m][:])
+                else:
+                    nc.vector.tensor_scalar(result[:], products[h][m][:], biases[m][:], 0.0, ALU.add, ALU.max)
+                nc.sync.dma_start(out[m * P:(m + 1) * P, h * half:(h + 1) * half], result[:])

@@ -6,7 +6,7 @@ ACT = mybir.ActivationFunctionType
 
 P = 128
 GROUP = 16
-HALVES = 2
+PIECES = 4
 FLOPS = 2 * 256 * 256 * 512
 
 
@@ -16,10 +16,10 @@ def tile_lookup_pool_max_relu_kernel(tc, tab, x0, w, b, offs, out):
     points = x0.shape[1]
     features = w.shape[1]
     row_blocks, feature_blocks = rows // P, features // P
-    piece_cols = points // GROUP
-    neighbours = offs.shape[1] // piece_cols
+    list_cols = points // GROUP
+    neighbours = offs.shape[1] // list_cols
 
-    half = points // HALVES
+    piece = points // PIECES
     last_block = row_blocks - 1
 
     with (
@@ -43,31 +43,33 @@ def tile_lookup_pool_max_relu_kernel(tc, tab, x0, w, b, offs, out):
             nc.sync.dma_start(bias[:], b[m * P:(m + 1) * P, :])
             biases.append(bias)
 
-        products = [[psum.tile([P, half], F32, name=f"product{h}_{m}") for m in range(feature_blocks)]
-                    for h in range(HALVES)]
+        products = [[psum.tile([P, piece], F32, name=f"product{m}_{c}") for c in range(PIECES)]
+                    for m in range(feature_blocks)]
         for r in range(row_blocks):
-            running = centres[r]
+            larger = []
             for d in range(neighbours):
-                larger = held.tile([P, points], F32, name=f"larger{r}_{d}")
-                picked = windows[r][:].indirect(offsets[:, d * piece_cols:(d + 1) * piece_cols])
-                nc.vector.tensor_tensor(larger[:], picked, running[:], ALU.max)
-                running = larger
-            for h in range(HALVES):
-                pooled = held.tile([P, half], BF16, name=f"pooled{r}_{h}")
-                source = running[:, h * half:(h + 1) * half]
+                best = held.tile([P, points], F32, name=f"larger{r}_{d}")
+                other = larger[-1] if larger and r != last_block else centres[r]
+                picked = windows[r][:].indirect(offsets[:, d * list_cols:(d + 1) * list_cols])
+                nc.vector.tensor_tensor(best[:], picked, other[:], ALU.max)
+                larger.append(best)
+            pooled = []
+            for c in range(PIECES):
+                rounded = held.tile([P, piece], BF16, name=f"pooled{r}_{c}")
+                cols = slice(c * piece, (c + 1) * piece)
                 if r == last_block:
-                    nc.vector.tensor_copy(pooled[:], source)
+                    nc.vector.tensor_tensor(rounded[:], larger[0][:, cols], larger[1][:, cols], ALU.max)
                 else:
-                    nc.scalar.copy(pooled[:], source)
-                for m in range(feature_blocks):
-                    nc.tensor.matmul(products[h][m][:], weights[:, r, m * P:(m + 1) * P], pooled[:],
+                    nc.scalar.copy(rounded[:], larger[-1][:, cols])
+                pooled.append(rounded)
+            for m in range(feature_blocks):
+                for c in range(PIECES):
+                    nc.tensor.matmul(products[m][c][:], weights[:, r, m * P:(m + 1) * P], pooled[c][:],
                                      start=(r == 0), stop=(r == last_block))
 
-        for h in range(HALVES):
-            for m in range(feature_blocks):
-                result = held.tile([P, half], F32, name=f"result{h}_{m}")
-                if m % 2 == 0:
-                    nc.scalar.activation(result[:], products[h][m][:], ACT.Relu, bias=biases[m][:])
-                else:
-                    nc.vector.tensor_scalar(result[:], products[h][m][:], biases[m][:], 0.0, ALU.add, ALU.max)
-                nc.sync.dma_start(out[m * P:(m + 1) * P, h * half:(h + 1) * half], result[:])
+        for m in range(feature_blocks):
+            for c in range(0, PIECES, 2):
+                result = held.tile([P, 2 * piece], F32, name=f"result{m}_{c}")
+                nc.scalar.activation(result[:, :piece], products[m][c][:], ACT.Relu, bias=biases[m][:])
+                nc.vector.tensor_scalar(result[:, piece:], products[m][c + 1][:], biases[m][:], 0.0, ALU.add, ALU.max)
+                nc.sync.dma_start(out[m * P:(m + 1) * P, c * piece:(c + 2) * piece], result[:])

import concourse.mybir as mybir

F32, BF16, U16 = mybir.dt.float32, mybir.dt.bfloat16, mybir.dt.uint16
ALU = mybir.AluOpType
ACT = mybir.ActivationFunctionType

P = 128
GROUP = 16
PIECES = 4
FLOPS = 2 * 256 * 256 * 512


def tile_lookup_pool_max_relu_kernel(tc, tab, x0, w, b, offs, out):
    nc = tc.nc
    rows, width = tab.shape
    points = x0.shape[1]
    features = w.shape[1]
    row_blocks, feature_blocks = rows // P, features // P
    list_cols = points // GROUP
    neighbours = offs.shape[1] // list_cols

    piece = points // PIECES
    last_block = row_blocks - 1

    with (
        tc.tile_pool(name="held", bufs=1) as held,
        tc.psum_pool(name="psum", bufs=1) as psum,
    ):
        windows = [held.tile([P, width], F32, name=f"window{r}") for r in range(row_blocks)]
        centres = [held.tile([P, points], F32, name=f"centre{r}") for r in range(row_blocks)]
        offsets = held.tile([P, offs.shape[1]], U16, name="offsets")
        nc.sync.dma_start(windows[0][:], tab[0:P, :])
        nc.sync.dma_start(offsets[:], offs)
        nc.sync.dma_start(centres[0][:], x0[0:P, :])
        for r in range(1, row_blocks):
            nc.sync.dma_start(windows[r][:], tab[r * P:(r + 1) * P, :])
            nc.sync.dma_start(centres[r][:], x0[r * P:(r + 1) * P, :])
        weights = held.tile([P, row_blocks, features], BF16, name="weights")
        nc.sync.dma_start(weights[:], w.rearrange("(r p) m -> p r m", p=P))
        biases = []
        for m in range(feature_blocks):
            bias = held.tile([P, 1], F32, name=f"bias{m}")
            nc.sync.dma_start(bias[:], b[m * P:(m + 1) * P, :])
            biases.append(bias)

        products = [[psum.tile([P, piece], F32, name=f"product{m}_{c}") for c in range(PIECES)]
                    for m in range(feature_blocks)]
        for r in range(row_blocks):
            larger = []
            for d in range(neighbours):
                best = held.tile([P, points], F32, name=f"larger{r}_{d}")
                other = larger[-1] if larger and r != last_block else centres[r]
                picked = windows[r][:].indirect(offsets[:, d * list_cols:(d + 1) * list_cols])
                nc.vector.tensor_tensor(best[:], picked, other[:], ALU.max)
                larger.append(best)
            pooled = []
            for c in range(PIECES):
                rounded = held.tile([P, piece], BF16, name=f"pooled{r}_{c}")
                cols = slice(c * piece, (c + 1) * piece)
                if r == last_block:
                    nc.vector.tensor_tensor(rounded[:], larger[0][:, cols], larger[1][:, cols], ALU.max)
                else:
                    nc.scalar.copy(rounded[:], larger[-1][:, cols])
                pooled.append(rounded)
            for m in range(feature_blocks):
                for c in range(PIECES):
                    nc.tensor.matmul(products[m][c][:], weights[:, r, m * P:(m + 1) * P], pooled[c][:],
                                     start=(r == 0), stop=(r == last_block))

        for m in range(feature_blocks):
            for c in range(0, PIECES, 2):
                result = held.tile([P, 2 * piece], F32, name=f"result{m}_{c}")
                nc.scalar.activation(result[:, :piece], products[m][c][:], ACT.Relu, bias=biases[m][:])
                nc.vector.tensor_scalar(result[:, piece:], products[m][c + 1][:], biases[m][:], 0.0, ALU.add, ALU.max)
                nc.sync.dma_start(out[m * P:(m + 1) * P, c * piece:(c + 2) * piece], result[:])
